import numpy as np, ml_dtypes
CORES = [24,40,56,80,88,96]
N = 6
import mx_ref
NC, D = 128, 2
SRC = [[0,4],[0,2],[1,3],[1,5],[1,4],[3,5]]
BF = ml_dtypes.bfloat16
def setup_inputs(rng):
    def f(*shape):
        return mx_ref.flush((rng.standard_normal(shape, dtype=np.float32) * np.exp2(rng.integers(-2, 3, shape[:-1] + (1,)))).astype(BF))
    return {"w": f(N, 128, D * 512), "x": f(N, 128, 4 * NC)}
def setup_inputs_blocks(rng):
    d = setup_inputs(rng)
    for k in ("w", "x"): d[k] = mx_ref.spread(d[k], rng, 1)
    return d
def setup_inputs_wide(rng):
    d = setup_inputs(rng)
    for k in ("w", "x"): d[k] = mx_ref.flush((d[k].astype(np.float32) * np.exp2(rng.integers(-8, 9, (N, 1, 1))).astype(np.float32)).astype(BF))
    return d
def setup_inputs_zeros(rng):
    d = setup_inputs(rng); v = d["x"].reshape(N, 128, -1, 4).copy()
    v[np.broadcast_to((rng.random((N, 1, v.shape[2], 1)) < 0.33), v.shape)] = 0
    d["x"] = v.reshape(d["x"].shape)
    return d
def reference(w, x):
    QX = [mx_ref.quantize(x[j]) for j in range(N)]
    y = np.zeros((N, 128, NC), np.float32)
    for r in range(N):
        for i in range(D):
            p = mx_ref.matmul(mx_ref.quantize(w[r][:, 512 * i:512 * i + 512]), QX[SRC[r][i]])
            y[r] = p if i == 0 else y[r] + p
    return {"y": y}

from concourse.bass import DstId, RemoteDMATransfer
from concourse.mybir import dt

NC = 128
D = 2

SCRATCH = {
    "xb": ("sbuf", [128, 4 * NC], "bfloat16"),
    "wb": ("sbuf", [128, 4 * NC * D], "bfloat16"),
    "xc": ("sbuf", [128, NC], "float8_e4m3fn_x4"),
    "xs": ("sbuf", [128, NC], "uint8"),
    "wc": ("sbuf", [128, NC * D], "float8_e4m3fn_x4"),
    "ws": ("sbuf", [128, NC * D], "uint8"),
    "c0": ("sbuf", [128, NC], "float8_e4m3fn_x4"),
    "s0": ("sbuf", [128, NC], "uint8"),
    "c1": ("sbuf", [128, NC], "float8_e4m3fn_x4"),
    "s1": ("sbuf", [128, NC], "uint8"),
    "acc": ("psum", [128, 512], "float32"),
    "yb": ("sbuf", [128, NC], "float32"),
}
SEMAPHORES = ["xl", "wl", "xq", "wq", "in0", "in1", "sent", "mm", "ev", "st"]

K_HOP1 = 8
K_HOP2 = 4
K_DIRECT = 8


def _bits(mask):
    return [e for e in range(mask.bit_length()) if (mask >> e) & 1]


def _mask_of(engines):
    m = 0
    for e in engines:
        m |= 1 << e
    return m


def _pow2_at_most(n):
    p = 1
    while 2 * p <= n:
        p *= 2
    return p


def _thin(engines, k):
    k = min(k, _pow2_at_most(len(engines)))
    return engines[::len(engines) // k][:k]


def _plan(T, topo):
    cores = list(T.cores)
    src = T.tables["SRC"]
    taken = set(cores)
    relay = {c: [] for c in cores}
    direct = {c: [] for c in cores}
    jobs = {}
    how = {}
    for j, s in enumerate(cores):
        for r, d in enumerate(cores):
            for i, jj in enumerate(src[r]):
                if jj != j:
                    continue
                if r == j:
                    how[(r, i)] = 0
                elif topo.may_write(s, d):
                    how[(r, i)] = 1
                    direct[s].append((d, i))
                else:
                    how[(r, i)] = 2
                    near = [h for h in range(topo.CHIPS * topo.CORES_PER_CHIP)
                            if topo.chip(h) == topo.chip(s) and h not in taken and topo.may_write(h, d)]
                    near.sort(key=lambda h: (topo.die(h) != topo.die(s), h))
                    pair = near[:2]
                    taken.update(pair)
                    relay[s].append(tuple(pair))
                    for kind, h in enumerate(pair):
                        jobs[h] = (kind, d, i)
    return relay, direct, jobs, how


def _pool(core, relay, direct, topo):
    m = -1
    for pair in relay[core]:
        for h in pair:
            m &= topo.mask(core, h)
    for d, _ in direct[core]:
        m &= topo.mask(core, d)
    return _bits(m)


def _direct_engines(core, relay, direct, topo):
    pool = _thin(_pool(core, relay, direct, topo), K_DIRECT)
    n = len(direct[core])
    per = _pow2_at_most(len(pool) // n)
    return [pool[a * per:(a + 1) * per] for a in range(n)]


def _hop2_engines(h, d, topo):
    return _thin(_bits(topo.mask(h, d)), K_HOP2)


def _tile(T, kind, name):
    if kind == 0:
        return T["%sc" % name if name == "x" else "c%s" % name][:].bitcast(dt.uint8)
    return T["%ss" % name if name == "x" else "s%s" % name][:]


def _send(g, T, topo, in_ap, writes):
    if len(writes) == 1:
        d, out_ap, sem, engines = writes[0]
        rid, pid, _ = topo.addr(d)
        g.remote_dma(out_ap, in_ap, sem, T.sem.sent, pid, rid, _mask_of(engines))
        return len(engines)
    transfers = []
    for d, out_ap, sem, engines in writes:
        rid, pid, _ = topo.addr(d)
        transfers.append(RemoteDMATransfer(dst_ids=[DstId(rid=rid, pnc=pid)], dma_engine_mask=_mask_of(engines),
                                           remote_sem=sem, src=in_ap, dst=out_ap))
    g.remote_dma_fused(transfers, local_sem=T.sem.sent)
    return sum(len(w[3]) for w in writes)


def rank_program(g, core, T, topo):
    relay, direct, jobs, how = _plan(T, topo)
    cores = list(T.cores)
    rank = T.rank_of(core)

    if rank is None:
        if core not in jobs:
            return
        kind, d, slot = jobs[core]
        owner = [s for s in cores if any(core in pair for pair in relay[s])][0]
        k_in = len(_thin(_pool(owner, relay, direct, topo), K_HOP1))
        g.wait_ge(T.sem.in0, k_in)
        n = _send(g, T, topo, _tile(T, kind, "0"),
                  [(d, _tile(T, kind, "%d" % slot), T.sem["in%d" % slot], _hop2_engines(core, d, topo))])
        g.wait_ge(T.sem.sent, n)
        return

    g.sync.dma_start(T.xb[:], T.x[:]).then_inc(T.sem.xl, 16)
    g.sync.dma_start(T.wb[:], T.w[:]).then_inc(T.sem.wl, 16)

    g.vector.wait_ge(T.sem.xl, 16)
    g.vector.quantize_mx(T.xc[:], T.xs[:], T.xb[:]).then_inc(T.sem.xq, 1)
    g.vector.wait_ge(T.sem.wl, 16)
    g.vector.quantize_mx(T.wc[:], T.ws[:], T.wb[:]).then_inc(T.sem.wq, 1)

    sent = 0
    if relay[core] or direct[core]:
        g.wait_ge(T.sem.xq, 1)
        pool = _pool(core, relay, direct, topo)
        for pair in relay[core]:
            for kind, h in enumerate(pair):
                sent += _send(g, T, topo, _tile(T, kind, "x"),
                              [(h, _tile(T, kind, "0"), T.sem.in0, _thin(pool, K_HOP1))])
        if direct[core]:
            groups = _direct_engines(core, relay, direct, topo)
            for kind in range(2):
                sent += _send(g, T, topo, _tile(T, kind, "x"),
                              [(d, _tile(T, kind, "%d" % i), T.sem["in%d" % i], e)
                               for (d, i), e in zip(direct[core], groups)])

    order = sorted(range(D), key=lambda i: how[(rank, i)])
    g.tensor.wait_ge(T.sem.wq, 1)
    for n, i in enumerate(order):
        owner = cores[T.tables["SRC"][rank][i]]
        if how[(rank, i)] == 0:
            g.tensor.wait_ge(T.sem.xq, 1)
            rc, rs = T.xc[:], T.xs[:]
        else:
            if how[(rank, i)] == 1:
                a = direct[owner].index((core, i))
                k = 2 * len(_direct_engines(owner, relay, direct, topo)[a])
            else:
                k = sum(len(_hop2_engines(h, core, topo)) for h, job in jobs.items() if job[1:] == (core, i))
            g.tensor.wait_ge(T.sem["in%d" % i], k)
            rc, rs = T["c%d" % i][:], T["s%d" % i][:]
        mm = g.tensor.matmul_mx(T.acc[:, 0:NC], T.wc[:, NC * i:NC * (i + 1)], T.ws[:, NC * i:NC * (i + 1)],
                                rc, rs, n == 0, n == D - 1)
    mm.then_inc(T.sem.mm, 1)

    g.vector.wait_ge(T.sem.mm, 1)
    g.vector.tensor_copy(T.yb[:], T.acc[:, 0:NC]).then_inc(T.sem.ev, 1)
    g.sync.wait_ge(T.sem.ev, 1)
    g.sync.dma_start(T.y[:], T.yb[:]).then_inc(T.sem.st, 16)
    g.sync.wait_ge(T.sem.st, 16)
    if sent:
        g.wait_ge(T.sem.sent, sent)
